import numpy as np, ml_dtypes
CORES = [1,14,19,24,37,42,55,60,65,78,83,88,101,106,119,124]
N = 16
T = 512
def entries(a): return a.T.reshape(-1)
def pack(v, P): return np.ascontiguousarray(np.asarray(v, np.int32).reshape(-1, P).T)
def lists(rng, how):
    Q = rng.permutation(N * T)
    if how == "stay": Q = np.arange(N * T)
    if how == "own": Q = np.concatenate([T * r + rng.permutation(T) for r in range(N)])
    if how == "shift": Q = (np.arange(N * T) + T * int(rng.integers(1, N)) + 1) % (N * T)
    if how == "deal": Q = (np.arange(N * T) % N) * T + np.arange(N * T) // N
    if how == "block": s = int(rng.integers(1, N)); Q = np.concatenate([T * ((r + s) % N) + rng.permutation(T) for r in range(N)])
    return {"goes": np.broadcast_to(pack(Q, 16), (N, 16, N * T // 16)).copy()}
def setup_inputs(rng):
    return dict({"x": rng.standard_normal((N, 128, T), dtype=np.float32).astype(ml_dtypes.bfloat16)}, **lists(rng, "uniform"))
def setup_inputs_block(rng):
    d = setup_inputs(rng); d.update(lists(rng, "block"))
    for k in ("x",): d[k] = (d[k].astype(np.float32) * 1048576.0).astype(d[k].dtype)
    return d
def setup_inputs_deal(rng):
    d = setup_inputs(rng); d.update(lists(rng, "deal"))
    for k in ("x",): d[k] = (d[k].astype(np.float32) * (1 / 1024.0)).astype(d[k].dtype)
    return d
def setup_inputs_own(rng):
    d = setup_inputs(rng); d.update(lists(rng, "own"))
    return d
def setup_inputs_shift(rng):
    d = setup_inputs(rng); d.update(lists(rng, "shift"))
    return d
def setup_inputs_stay(rng):
    d = setup_inputs(rng); d.update(lists(rng, "stay"))
    return d
def check_inputs(x):
    bad = []
    if x["goes"].min() < 0 or x["goes"].max() >= N * T: bad.append("goes out of range")
    if not np.array_equal(np.sort(entries(x["goes"][0])), np.arange(N * T)): bad.append("goes isn't a permutation")
    if not all(np.array_equal(a, x["goes"][0]) for a in x["goes"]): bad.append("goes isn't alike on all ranks")
    return bad
def reference(x, goes):
    A = np.concatenate(list(x), axis=1); Y = np.zeros_like(A)
    Y[:, entries(goes[0])] = A
    return {"y": np.stack([Y[:, T * r:T * r + T] for r in range(N)])}

@@ -1,0 +1,218 @@
+from concourse.bass import DstId, RemoteDMATransfer
+from concourse.mybir import AluOpType
+
+W = 512
+TL = 32
+MW = W + TL
+
+SCRATCH = {
+    "win": ("sbuf", [128, 4 * W], "bfloat16"),
+    "snd": ("sbuf", [128, 3 * MW], "bfloat16"),
+    "cnd": ("sbuf", [128, 4 * MW], "bfloat16"),
+    "ysb": ("sbuf", [128, W], "bfloat16"),
+    "swn": ("sbuf", [128, 16 * W], "bfloat16"),
+    "gin": ("sbuf", [128, 16], "int32"),
+    "gof": ("sbuf", [128, 16], "uint16"),
+    "pix": ("sbuf", [128, 1], "int32"),
+    "cin": ("sbuf", [128, 2], "int32"),
+    "cfl": ("sbuf", [128, 8], "float32"),
+    "jj1": ("sbuf", [128, 256], "bfloat16"),
+    "msk": ("sbuf", [128, 128], "float32"),
+    "rpl": ("sbuf", [128, 128], "float32"),
+    "iqq": ("sbuf", [128, TL], "float32"),
+    "val": ("sbuf", [128, 256], "bfloat16"),
+    "wgt": ("sbuf", [128, 8], "bfloat16"),
+    "rr1": ("sbuf", [128, 128], "float32"),
+    "lof": ("sbuf", [128, 128], "uint16"),
+    "fof": ("sbuf", [128, TL], "uint16"),
+    "px1": ("psum", [128, 512], "float32"),
+    "pl1": ("psum", [128, 512], "float32"),
+}
+SEMAPHORES = ["ldx", "ldg", "gip", "gij", "gia", "gim", "giq", "vv", "pe", "p1", "q1", "q2", "q3", "hin", "sent", "st"]
+
+
+def _bits(m):
+    return bin(m).count("1")
+
+
+def _plan(T, topo):
+    cores = list(T.cores)
+    n = len(cores)
+    plane0 = [r for r in range(n) if r == 0 or topo.same_plane(topo.chip(cores[0]), topo.chip(cores[r]))]
+    plane1 = [r for r in range(n) if r not in plane0]
+    grid = [[plane0[2 * R], plane1[2 * R], plane0[2 * R + 1], plane1[2 * R + 1]] for R in range(4)]
+    plan = {}
+    for R in range(4):
+        for C in range(4):
+            r = grid[R][C]
+            c = cores[r]
+            others = [grid[R][k] for k in range(4) if k != C]
+            direct = [o for o in others if topo.may_write(c, cores[o])]
+            relay = [o for o in others if o not in direct]
+            helpers = []
+            if relay:
+                chip = topo.chip(c)
+                cand = [h for h in range(128) if topo.chip(h) == chip and h != c
+                        and all(topo.may_write(h, cores[o]) for o in relay)]
+                cand.sort(key=lambda h: (topo.die(h) != topo.die(c), h))
+                helpers = cand[:2]
+            plan[r] = dict(R=R, C=C, direct=direct, relay=relay, helpers=helpers)
+    return grid, plan
+
+
+def _multi(T, topo, src_core, dst_ranks, ap, sem):
+    cores = T.cores
+    m = topo.mask(src_core, cores[dst_ranks[0]])
+    ids = []
+    for o in dst_ranks:
+        m &= topo.mask(src_core, cores[o])
+        rid, pid, _s = topo.addr(cores[o])
+        ids.append(DstId(rid=rid, pnc=pid))
+    return RemoteDMATransfer(dst_ids=ids, dma_engine_mask=m, remote_sem=sem, srcs=[ap],
+                             dsts=[ap for _o in dst_ranks]), _bits(m)
+
+
+def rank_program(g, core, T, topo):
+    grid, plan = _plan(T, topo)
+    cores = T.cores
+    S = T.sem
+    rank = T.rank_of(core)
+
+    if rank is None:
+        for r, pl in plan.items():
+            for h, hc in enumerate(pl["helpers"]):
+                if hc != core:
+                    continue
+                lo = topo.mask(cores[r], cores[pl["relay"][0]])
+                inm = lo if h == 0 else topo.mask(cores[r], hc) & ~lo
+                a = W * pl["C"] + (W // 2) * h
+                tr, nb = _multi(T, topo, core, pl["relay"], T.win[:, a:a + W // 2], S.p1)
+                g.wait_ge(S.hin, _bits(inm))
+                g.remote_dma_fused([tr], local_sem=S.sent)
+                g.wait_ge(S.sent, nb)
+        return
+
+    me = plan[rank]
+    R, C = me["R"], me["C"]
+    V = g.vector
+    A = AluOpType
+    nv = [0]
+
+    def vop(inst):
+        inst.then_inc(S.vv, 1)
+        nv[0] += 1
+        V.wait_ge(S.vv, nv[0])
+        return nv[0]
+
+    own = T.win[:, W * C:W * C + W]
+    g.sync.dma_start(own, T.x[:, :]).then_inc(S.ldx, 16)
+    for grp in range(8):
+        s = grid[R][grp >> 1]
+        c0 = 32 * s + 16 * (grp & 1)
+        g.scalar.dma_start(T.gin[16 * grp:16 * grp + 16, :], T.goes[:, c0:c0 + 16]).then_inc(S.ldg, 16)
+
+    g.iota(T.pix[:, 0:1], [[0, 1]], 0, 1).then_inc(S.gip, 1)
+    g.iota(T.jj1[:, :], [[1, 256]], 1, 0, allow_small_or_imprecise_dtypes=True).then_inc(S.gij, 1)
+    g.iota(T.msk[:, :], [[0, 16], [1, 8]], 0, 0, allow_small_or_imprecise_dtypes=True).then_inc(S.gia, 1)
+    g.iota(T.rpl[:, :], [[0, 8], [1, 16]], 0, 0, allow_small_or_imprecise_dtypes=True).then_inc(S.gim, 1)
+    g.iota(T.iqq[:, :], [[16, TL]], 0, 0, allow_small_or_imprecise_dtypes=True).then_inc(S.giq, 1)
+
+    sent = 0
+    g.wait_ge(S.ldx, 16)
+    if me["relay"]:
+        lo = topo.mask(core, cores[me["relay"][0]])
+        trs = []
+        for h, hc in enumerate(me["helpers"]):
+            m = lo if h == 0 else topo.mask(core, hc) & ~lo
+            rid, pid, _s = topo.addr(hc)
+            a = W * C + (W // 2) * h
+            trs.append(RemoteDMATransfer(dst_ids=[DstId(rid=rid, pnc=pid)], dma_engine_mask=m, remote_sem=S.hin,
+                                         src=T.win[:, a:a + W // 2], dst=T.win[:, a:a + W // 2]))
+            sent += _bits(m)
+        g.remote_dma_fused(trs, local_sem=S.sent)
+    tr, nb = _multi(T, topo, core, me["direct"], own, S.p1)
+    g.remote_dma_fused([tr], local_sem=S.sent)
+    sent += nb
+
+    p1 = 0
+    for k in range(4):
+        o = grid[R][k]
+        if o == rank:
+            continue
+        if rank in plan[o]["direct"]:
+            p1 += _bits(topo.mask(cores[o], core))
+        else:
+            p1 += sum(_bits(topo.mask(hc, core)) for hc in plan[o]["helpers"])
+
+    pg, pr, e0, e1, t0, s1 = (T.cfl[:, i:i + 1] for i in range(6))
+    for Rp in range(4):
+        a = W * grid[Rp][C]
+        vop(V.memset(T.swn[:, a:a + W], 0.0))
+    V.wait_ge(S.gip, 1)
+    vop(V.tensor_scalar(T.cin[:, 0:1], T.pix[:, 0:1], 4, None, A.arith_shift_right))
+    vop(V.tensor_scalar(T.cin[:, 1:2], T.pix[:, 0:1], 15, None, A.bitwise_and))
+    vop(V.tensor_copy(pg, T.cin[:, 0:1]))
+    vop(V.tensor_copy(pr, T.cin[:, 1:2]))
+    vop(V.tensor_scalar(e0, pr, 0.0, None, A.is_equal))
+    vop(V.tensor_scalar(e1, pr, 1.0, None, A.is_equal))
+    V.wait_ge(S.gij, 1)
+    vop(V.tensor_scalar(T.val[:, :], T.jj1[:, :], e0, e1, A.mult, A.add))
+    vop(V.tensor_scalar(t0, pg, 256.0, e1, A.mult, A.mult))
+    vop(V.tensor_tensor(s1, t0, e0, A.add))
+    vop(V.tensor_scalar(T.wgt[:, :], T.jj1[:, 0:8], 0.0, s1, A.mult, A.add))
+    V.wait_ge(S.ldg, 128)
+    vop(V.tensor_copy(T.gof[:, :], T.gin[:, :]))
+    n_sc = vop(V.tensor_copy(T.swn[:, 0:16 * W].indirect(T.gof[:, 0:16]), T.val[:, :]))
+    V.wait_ge(S.gia, 1)
+    vop(V.tensor_scalar(T.msk[:, :], T.msk[:, :], pg, None, A.is_equal))
+    V.wait_ge(S.gim, 1)
+    vop(V.tensor_scalar(T.rpl[:, :], T.rpl[:, :], pr, None, A.is_equal))
+    V.wait_ge(S.giq, 1)
+    vop(V.tensor_scalar(T.iqq[:, :], T.iqq[:, :], pr, None, A.add))
+
+    g.tensor.wait_ge(S.vv, n_sc)
+    for Rp in range(4):
+        for u4 in range(4):
+            u = 4 * Rp + u4
+            a = W * grid[Rp][C] + 128 * u4
+            g.tensor.matmul(T.px1[:, 8 * u:8 * u + 8], T.swn[:, a:a + 128], T.wgt[:, :], True, True).then_inc(S.pe, 1)
+    V.wait_ge(S.pe, 16)
+    n_r1 = vop(V.tensor_tensor(T.rr1[:, :], T.px1[:, 0:128], T.msk[:, :], A.mult))
+    g.tensor.wait_ge(S.vv, n_r1)
+    g.tensor.matmul(T.pl1[:, 0:128], T.rpl[:, :], T.rr1[:, :], True, True).then_inc(S.pe, 1)
+    V.wait_ge(S.pe, 17)
+    vop(V.tensor_scalar(T.lof[:, :], T.pl1[:, 0:128], -1.0, 0.0, A.add, A.max))
+    for d in (1, 2, 3):
+        Rp = (R + d) % 4
+        a = MW * (d - 1) + W
+        vop(V.tensor_scalar(T.snd[:, a:a + TL], T.pl1[:, TL * Rp:TL * Rp + TL], 0.5, float(MW * R), A.is_gt, A.mult))
+    a = MW * R + W
+    vop(V.tensor_scalar(T.cnd[:, a:a + TL], T.pl1[:, TL * R:TL * R + TL], 0.5, float(MW * R), A.is_gt, A.mult))
+    vop(V.tensor_tensor(T.iqq[:, :], T.iqq[:, :], T.cnd[:, a:a + TL], A.add))
+
+    V.wait_ge(S.ldx, 16)
+    V.wait_ge(S.p1, p1)
+    for d in (1, 2, 3):
+        Rp = (R + d) % 4
+        a = MW * (d - 1)
+        n_g = vop(V.tensor_copy(T.snd[:, a:a + W], T.win[:, 0:4 * W].indirect(T.lof[:, TL * Rp:TL * Rp + TL])))
+        dst = cores[grid[Rp][C]]
+        rid, pid, _s = topo.addr(dst)
+        m = topo.mask(core, dst)
+        g.wait_ge(S.vv, n_g)
+        g.remote_dma(out_ap=T.cnd[:, MW * R:MW * R + MW], in_ap=T.snd[:, a:a + MW], remote_sem=S["q%d" % d],
+                     local_sem=S.sent, pid=pid, routing_id=rid, dma_engine_mask=m)
+        sent += _bits(m)
+    vop(V.tensor_copy(T.cnd[:, MW * R:MW * R + W], T.win[:, 0:4 * W].indirect(T.lof[:, TL * R:TL * R + TL])))
+
+    for d in (1, 2, 3):
+        Rs = (R - d) % 4
+        V.wait_ge(S["q%d" % d], _bits(topo.mask(cores[grid[Rs][C]], core)))
+        a = MW * Rs + W
+        vop(V.tensor_tensor(T.iqq[:, :], T.iqq[:, :], T.cnd[:, a:a + TL], A.add))
+    vop(V.tensor_copy(T.fof[:, :], T.iqq[:, :]))
+    n_y = vop(V.tensor_copy(T.ysb[:, :], T.cnd[:, 0:4 * MW].indirect(T.fof[:, :])))
+    g.sync.wait_ge(S.vv, n_y)
+    g.sync.dma_start(T.y[:, :], T.ysb[:, :]).then_inc(S.st, 16)
+    g.sync.wait_ge(S.st, 16)
+    g.wait_ge(S.sent, sent)

@@ -28,11 +28,27 @@ SCRATCH = {
     "px1": ("psum", [128, 512], "float32"),
     "pl1": ("psum", [128, 512], "float32"),
 }
-SEMAPHORES = ["ldx", "ldg", "gip", "gij", "gia", "gim", "giq", "vv", "pe", "p1", "q1", "q2", "q3", "hin", "sent", "st"]
+SEMAPHORES = ["ldx", "ldg", "gip", "gij", "gia", "gim", "giq", "vv", "pe", "p1", "q1", "q2", "q3", "hin", "sent", "st",
+              "st2"]
 
 
 def _bits(m):
     return bin(m).count("1")
+
+
+def _half(m):
+    keep = _bits(m) // 2
+    out = 0
+    for b in range(16):
+        if (m >> b) & 1 and keep > 0:
+            out |= 1 << b
+            keep -= 1
+    return out
+
+
+def _mask2(topo, src, dst, d):
+    m = topo.mask(src, dst)
+    return _half(m) if d == 1 else (m & ~_half(m) if d == 2 else m)
 
 
 def _plan(T, topo):
@@ -94,14 +110,16 @@ def rank_program(g, core, T, topo):
 
     me = plan[rank]
     R, C = me["R"], me["C"]
+    RL = (R + 1) % 4
     V = g.vector
     A = AluOpType
     nv = [0]
 
-    def vop(inst):
+    def vop(inst, wait=True):
         inst.then_inc(S.vv, 1)
         nv[0] += 1
-        V.wait_ge(S.vv, nv[0])
+        if wait:
+            V.wait_ge(S.vv, nv[0])
         return nv[0]
 
     own = T.win[:, W * C:W * C + W]
@@ -109,7 +127,8 @@ def rank_program(g, core, T, topo):
     for grp in range(8):
         s = grid[R][grp >> 1]
         c0 = 32 * s + 16 * (grp & 1)
-        g.scalar.dma_start(T.gin[16 * grp:16 * grp + 16, :], T.goes[:, c0:c0 + 16]).then_inc(S.ldg, 16)
+        q = g.scalar if grp % 2 == 0 else g.sync
+        q.dma_start(T.gin[16 * grp:16 * grp + 16, :], T.goes[:, c0:c0 + 16]).then_inc(S.ldg, 16)
 
     g.iota(T.pix[:, 0:1], [[0, 1]], 0, 1).then_inc(S.gip, 1)
     g.iota(T.jj1[:, :], [[1, 256]], 1, 0, allow_small_or_imprecise_dtypes=True).then_inc(S.gij, 1)
@@ -147,28 +166,28 @@ def rank_program(g, core, T, topo):
     pg, pr, e0, e1, t0, s1 = (T.cfl[:, i:i + 1] for i in range(6))
     for Rp in range(4):
         a = W * grid[Rp][C]
-        vop(V.memset(T.swn[:, a:a + W], 0.0))
+        vop(V.memset(T.swn[:, a:a + W], 0.0), wait=False)
     V.wait_ge(S.gip, 1)
-    vop(V.tensor_scalar(T.cin[:, 0:1], T.pix[:, 0:1], 4, None, A.arith_shift_right))
+    vop(V.tensor_scalar(T.cin[:, 0:1], T.pix[:, 0:1], 4, None, A.arith_shift_right), wait=False)
     vop(V.tensor_scalar(T.cin[:, 1:2], T.pix[:, 0:1], 15, None, A.bitwise_and))
-    vop(V.tensor_copy(pg, T.cin[:, 0:1]))
+    vop(V.tensor_copy(pg, T.cin[:, 0:1]), wait=False)
     vop(V.tensor_copy(pr, T.cin[:, 1:2]))
-    vop(V.tensor_scalar(e0, pr, 0.0, None, A.is_equal))
+    vop(V.tensor_scalar(e0, pr, 0.0, None, A.is_equal), wait=False)
     vop(V.tensor_scalar(e1, pr, 1.0, None, A.is_equal))
     V.wait_ge(S.gij, 1)
-    vop(V.tensor_scalar(T.val[:, :], T.jj1[:, :], e0, e1, A.mult, A.add))
+    vop(V.tensor_scalar(T.val[:, :], T.jj1[:, :], e0, e1, A.mult, A.add), wait=False)
     vop(V.tensor_scalar(t0, pg, 256.0, e1, A.mult, A.mult))
     vop(V.tensor_tensor(s1, t0, e0, A.add))
-    vop(V.tensor_scalar(T.wgt[:, :], T.jj1[:, 0:8], 0.0, s1, A.mult, A.add))
+    vop(V.tensor_scalar(T.wgt[:, :], T.jj1[:, 0:8], 0.0, s1, A.mult, A.add), wait=False)
     V.wait_ge(S.ldg, 128)
     vop(V.tensor_copy(T.gof[:, :], T.gin[:, :]))
     n_sc = vop(V.tensor_copy(T.swn[:, 0:16 * W].indirect(T.gof[:, 0:16]), T.val[:, :]))
     V.wait_ge(S.gia, 1)
-    vop(V.tensor_scalar(T.msk[:, :], T.msk[:, :], pg, None, A.is_equal))
+    vop(V.tensor_scalar(T.msk[:, :], T.msk[:, :], pg, None, A.is_equal), wait=False)
     V.wait_ge(S.gim, 1)
-    vop(V.tensor_scalar(T.rpl[:, :], T.rpl[:, :], pr, None, A.is_equal))
+    vop(V.tensor_scalar(T.rpl[:, :], T.rpl[:, :], pr, None, A.is_equal), wait=False)
     V.wait_ge(S.giq, 1)
-    vop(V.tensor_scalar(T.iqq[:, :], T.iqq[:, :], pr, None, A.add))
+    vop(V.tensor_scalar(T.iqq[:, :], T.iqq[:, :], pr, float(MW * RL), A.add, A.add))
 
     g.tensor.wait_ge(S.vv, n_sc)
     for Rp in range(4):
@@ -181,38 +200,48 @@ def rank_program(g, core, T, topo):
     g.tensor.wait_ge(S.vv, n_r1)
     g.tensor.matmul(T.pl1[:, 0:128], T.rpl[:, :], T.rr1[:, :], True, True).then_inc(S.pe, 1)
     V.wait_ge(S.pe, 17)
-    vop(V.tensor_scalar(T.lof[:, :], T.pl1[:, 0:128], -1.0, 0.0, A.add, A.max))
-    for d in (1, 2, 3):
-        Rp = (R + d) % 4
-        a = MW * (d - 1) + W
-        vop(V.tensor_scalar(T.snd[:, a:a + TL], T.pl1[:, TL * Rp:TL * Rp + TL], 0.5, float(MW * R), A.is_gt, A.mult))
-    a = MW * R + W
-    vop(V.tensor_scalar(T.cnd[:, a:a + TL], T.pl1[:, TL * R:TL * R + TL], 0.5, float(MW * R), A.is_gt, A.mult))
-    vop(V.tensor_tensor(T.iqq[:, :], T.iqq[:, :], T.cnd[:, a:a + TL], A.add))
+
+    def tail(out, Rp):
+        return V.tensor_scalar(out, T.pl1[:, TL * Rp:TL * Rp + TL], 0.5, float(MW * (R - (Rp + 1) % 4)),
+                               A.is_gt, A.mult)
+
+    vop(V.tensor_scalar(T.lof[:, :], T.pl1[:, 0:128], -1.0, 0.0, A.add, A.max), wait=False)
+    vop(tail(T.snd[:, W:MW], (R + 1) % 4))
 
     V.wait_ge(S.ldx, 16)
     V.wait_ge(S.p1, p1)
     for d in (1, 2, 3):
         Rp = (R + d) % 4
         a = MW * (d - 1)
+        if d == 2:
+            vop(tail(T.snd[:, a + W:a + MW], Rp), wait=False)
         n_g = vop(V.tensor_copy(T.snd[:, a:a + W], T.win[:, 0:4 * W].indirect(T.lof[:, TL * Rp:TL * Rp + TL])))
         dst = cores[grid[Rp][C]]
         rid, pid, _s = topo.addr(dst)
-        m = topo.mask(core, dst)
+        m = _mask2(topo, core, dst, d)
         g.wait_ge(S.vv, n_g)
-        g.remote_dma(out_ap=T.cnd[:, MW * R:MW * R + MW], in_ap=T.snd[:, a:a + MW], remote_sem=S["q%d" % d],
+        w = MW if d < 3 else W
+        g.remote_dma(out_ap=T.cnd[:, MW * R:MW * R + w], in_ap=T.snd[:, a:a + w], remote_sem=S["q%d" % d],
                      local_sem=S.sent, pid=pid, routing_id=rid, dma_engine_mask=m)
         sent += _bits(m)
+    a = MW * R + W
+    vop(V.memset(T.cnd[:, MW * RL + W:MW * RL + MW], 0.0), wait=False)
+    vop(tail(T.cnd[:, a:a + TL], R))
+    vop(V.tensor_tensor(T.iqq[:, :], T.iqq[:, :], T.cnd[:, a:a + TL], A.add), wait=False)
     vop(V.tensor_copy(T.cnd[:, MW * R:MW * R + W], T.win[:, 0:4 * W].indirect(T.lof[:, TL * R:TL * R + TL])))
 
-    for d in (1, 2, 3):
+    for d in (1, 2):
         Rs = (R - d) % 4
-        V.wait_ge(S["q%d" % d], _bits(topo.mask(cores[grid[Rs][C]], core)))
+        V.wait_ge(S["q%d" % d], _bits(_mask2(topo, cores[grid[Rs][C]], core, d)))
         a = MW * Rs + W
         vop(V.tensor_tensor(T.iqq[:, :], T.iqq[:, :], T.cnd[:, a:a + TL], A.add))
     vop(V.tensor_copy(T.fof[:, :], T.iqq[:, :]))
-    n_y = vop(V.tensor_copy(T.ysb[:, :], T.cnd[:, 0:4 * MW].indirect(T.fof[:, :])))
-    g.sync.wait_ge(S.vv, n_y)
-    g.sync.dma_start(T.y[:, :], T.ysb[:, :]).then_inc(S.st, 16)
-    g.sync.wait_ge(S.st, 16)
+    V.wait_ge(S.q3, _bits(_mask2(topo, cores[grid[RL][C]], core, 3)))
+    H = W // 2
+    for h, q, sem in ((0, g.sync, S.st), (1, g.scalar, S.st2)):
+        n_y = vop(V.tensor_copy(T.ysb[:, H * h:H * h + H],
+                                T.cnd[:, 0:4 * MW].indirect(T.fof[:, (TL // 2) * h:(TL // 2) * (h + 1)])))
+        q.wait_ge(S.vv, n_y)
+        q.dma_start(T.y[:, H * h:H * h + H], T.ysb[:, H * h:H * h + H]).then_inc(sem, 16)
+        q.wait_ge(sem, 16)
     g.wait_ge(S.sent, sent)

@@ -1,5 +1,5 @@
 from concourse.bass import DstId, RemoteDMATransfer
-from concourse.mybir import AluOpType
+from concourse.mybir import AluOpType, ActivationFunctionType
 
 W = 512
 TL = 32
@@ -29,7 +29,7 @@ SCRATCH = {
     "pl1": ("psum", [128, 512], "float32"),
 }
 SEMAPHORES = ["ldx", "ldg", "gip", "gij", "gia", "gim", "giq", "vv", "pe", "p1", "q1", "q2", "q3", "hin", "sent", "st",
-              "st2"]
+              "st2", "g1", "g2", "g3a", "g3b", "own", "y0", "y1"]
 
 
 def _bits(m):
@@ -48,7 +48,7 @@ def _half(m):
 
 def _mask2(topo, src, dst, d):
     m = topo.mask(src, dst)
-    return _half(m) if d == 1 else (m & ~_half(m) if d == 2 else m)
+    return _half(m) if d % 2 == 1 else m & ~_half(m)
 
 
 def _plan(T, topo):
@@ -112,6 +112,7 @@ def rank_program(g, core, T, topo):
     R, C = me["R"], me["C"]
     RL = (R + 1) % 4
     V = g.vector
+    SC = g.scalar
     A = AluOpType
     nv = [0]
 
@@ -132,9 +133,6 @@ def rank_program(g, core, T, topo):
 
     g.iota(T.pix[:, 0:1], [[0, 1]], 0, 1).then_inc(S.gip, 1)
     g.iota(T.jj1[:, :], [[1, 256]], 1, 0, allow_small_or_imprecise_dtypes=True).then_inc(S.gij, 1)
-    g.iota(T.msk[:, :], [[0, 16], [1, 8]], 0, 0, allow_small_or_imprecise_dtypes=True).then_inc(S.gia, 1)
-    g.iota(T.rpl[:, :], [[0, 8], [1, 16]], 0, 0, allow_small_or_imprecise_dtypes=True).then_inc(S.gim, 1)
-    g.iota(T.iqq[:, :], [[16, TL]], 0, 0, allow_small_or_imprecise_dtypes=True).then_inc(S.giq, 1)
 
     sent = 0
     g.wait_ge(S.ldx, 16)
@@ -152,6 +150,10 @@ def rank_program(g, core, T, topo):
     tr, nb = _multi(T, topo, core, me["direct"], own, S.p1)
     g.remote_dma_fused([tr], local_sem=S.sent)
     sent += nb
+
+    g.iota(T.msk[:, :], [[0, 16], [1, 8]], 0, 0, allow_small_or_imprecise_dtypes=True).then_inc(S.gia, 1)
+    g.iota(T.rpl[:, :], [[0, 8], [1, 16]], 0, 0, allow_small_or_imprecise_dtypes=True).then_inc(S.gim, 1)
+    g.iota(T.iqq[:, :], [[16, TL]], 0, 0, allow_small_or_imprecise_dtypes=True).then_inc(S.giq, 1)
 
     p1 = 0
     for k in range(4):
@@ -206,42 +208,63 @@ def rank_program(g, core, T, topo):
                                A.is_gt, A.mult)
 
     vop(V.tensor_scalar(T.lof[:, :], T.pl1[:, 0:128], -1.0, 0.0, A.add, A.max), wait=False)
-    vop(tail(T.snd[:, W:MW], (R + 1) % 4))
+    vop(tail(T.snd[:, W:MW], (R + 1) % 4), wait=False)
+    vop(tail(T.snd[:, MW + W:2 * MW], (R + 2) % 4), wait=False)
+    a = MW * R + W
+    vop(V.memset(T.cnd[:, MW * RL + W:MW * RL + MW], 0.0), wait=False)
+    n_l = vop(tail(T.cnd[:, a:a + TL], R))
+    vop(V.tensor_tensor(T.iqq[:, :], T.iqq[:, :], T.cnd[:, a:a + TL], A.add))
 
+    H, HT = W // 2, TL // 2
+    win = T.win[:, 0:4 * W]
+
+    def sgather(out, window, off, sem):
+        SC.activation(out, window.indirect(off), ActivationFunctionType.Copy, bias=-0.0, scale=1.0).then_inc(sem, 1)
+
+    R1, R2, R3 = (R + 1) % 4, (R + 2) % 4, (R + 3) % 4
     V.wait_ge(S.ldx, 16)
     V.wait_ge(S.p1, p1)
-    for d in (1, 2, 3):
-        Rp = (R + d) % 4
-        a = MW * (d - 1)
-        if d == 2:
-            vop(tail(T.snd[:, a + W:a + MW], Rp), wait=False)
-        n_g = vop(V.tensor_copy(T.snd[:, a:a + W], T.win[:, 0:4 * W].indirect(T.lof[:, TL * Rp:TL * Rp + TL])))
+    V.tensor_copy(T.snd[:, 0:W], win.indirect(T.lof[:, TL * R1:TL * R1 + TL])).then_inc(S.g1, 1)
+    V.tensor_copy(T.snd[:, 2 * MW:2 * MW + H], win.indirect(T.lof[:, TL * R3:TL * R3 + HT])).then_inc(S.g3a, 1)
+    SC.wait_ge(S.vv, n_l)
+    SC.wait_ge(S.ldx, 16)
+    SC.wait_ge(S.p1, p1)
+    sgather(T.snd[:, MW:MW + W], win, T.lof[:, TL * R2:TL * R2 + TL], S.g2)
+    sgather(T.snd[:, 2 * MW + H:2 * MW + W], win, T.lof[:, TL * R3 + HT:TL * R3 + TL], S.g3b)
+    sgather(T.cnd[:, MW * R:MW * R + W], win, T.lof[:, TL * R:TL * R + TL], S.own)
+
+    for rdy, Rp, a, b, w, d, q in ((S.g1, R1, 0, 0, MW, 1, S.q1), (S.g2, R2, MW, 0, MW, 2, S.q2),
+                                   (S.g3a, R3, 2 * MW, 0, H, 3, S.q3), (S.g3b, R3, 2 * MW + H, H, H, 4, S.q3)):
         dst = cores[grid[Rp][C]]
         rid, pid, _s = topo.addr(dst)
         m = _mask2(topo, core, dst, d)
-        g.wait_ge(S.vv, n_g)
-        w = MW if d < 3 else W
-        g.remote_dma(out_ap=T.cnd[:, MW * R:MW * R + w], in_ap=T.snd[:, a:a + w], remote_sem=S["q%d" % d],
+        g.wait_ge(rdy, 1)
+        g.remote_dma(out_ap=T.cnd[:, MW * R + b:MW * R + b + w], in_ap=T.snd[:, a:a + w], remote_sem=q,
                      local_sem=S.sent, pid=pid, routing_id=rid, dma_engine_mask=m)
         sent += _bits(m)
-    a = MW * R + W
-    vop(V.memset(T.cnd[:, MW * RL + W:MW * RL + MW], 0.0), wait=False)
-    vop(tail(T.cnd[:, a:a + TL], R))
-    vop(V.tensor_tensor(T.iqq[:, :], T.iqq[:, :], T.cnd[:, a:a + TL], A.add), wait=False)
-    vop(V.tensor_copy(T.cnd[:, MW * R:MW * R + W], T.win[:, 0:4 * W].indirect(T.lof[:, TL * R:TL * R + TL])))
 
+    nq = {}
     for d in (1, 2):
         Rs = (R - d) % 4
-        V.wait_ge(S["q%d" % d], _bits(_mask2(topo, cores[grid[Rs][C]], core, d)))
+        nq[d] = _bits(_mask2(topo, cores[grid[Rs][C]], core, d))
+        V.wait_ge(S["q%d" % d], nq[d])
         a = MW * Rs + W
         vop(V.tensor_tensor(T.iqq[:, :], T.iqq[:, :], T.cnd[:, a:a + TL], A.add))
-    vop(V.tensor_copy(T.fof[:, :], T.iqq[:, :]))
-    V.wait_ge(S.q3, _bits(_mask2(topo, cores[grid[RL][C]], core, 3)))
-    H = W // 2
-    for h, q, sem in ((0, g.sync, S.st), (1, g.scalar, S.st2)):
-        n_y = vop(V.tensor_copy(T.ysb[:, H * h:H * h + H],
-                                T.cnd[:, 0:4 * MW].indirect(T.fof[:, (TL // 2) * h:(TL // 2) * (h + 1)])))
-        q.wait_ge(S.vv, n_y)
-        q.dma_start(T.y[:, H * h:H * h + H], T.ysb[:, H * h:H * h + H]).then_inc(sem, 16)
-        q.wait_ge(sem, 16)
+    n_f = vop(V.tensor_copy(T.fof[:, :], T.iqq[:, :]))
+    nq[3] = _bits(_mask2(topo, cores[grid[RL][C]], core, 3)) + _bits(_mask2(topo, cores[grid[RL][C]], core, 4))
+    cnd = T.cnd[:, 0:4 * MW]
+    V.wait_ge(S.q3, nq[3])
+    V.wait_ge(S.own, 1)
+    V.tensor_copy(T.ysb[:, 0:H], cnd.indirect(T.fof[:, 0:HT])).then_inc(S.y0, 1)
+    g.sync.wait_ge(S.y0, 1)
+    g.sync.dma_start(T.y[:, 0:H], T.ysb[:, 0:H]).then_inc(S.st, 16)
+    g.sync.wait_ge(S.st, 16)
+    SC.wait_ge(S.vv, n_f)
+    for d in (1, 2, 3):
+        SC.wait_ge(S["q%d" % d], nq[d])
+    SC.wait_ge(S.own, 1)
+    sgather(T.ysb[:, H:W], cnd, T.fof[:, HT:TL], S.y1)
+    SC.wait_ge(S.y1, 1)
+    SC.dma_start(T.y[:, H:W], T.ysb[:, H:W]).then_inc(S.st2, 16)
+    SC.wait_ge(S.st2, 16)
     g.wait_ge(S.sent, sent)

from concourse.bass import DstId, RemoteDMATransfer
from concourse.mybir import AluOpType, ActivationFunctionType

W = 512
TL = 32
MW = W + TL

SCRATCH = {
    "win": ("sbuf", [128, 4 * W], "bfloat16"),
    "snd": ("sbuf", [128, 3 * MW], "bfloat16"),
    "cnd": ("sbuf", [128, 4 * MW], "bfloat16"),
    "ysb": ("sbuf", [128, W], "bfloat16"),
    "swn": ("sbuf", [128, 16 * W], "bfloat16"),
    "gin": ("sbuf", [128, 16], "int32"),
    "gof": ("sbuf", [128, 16], "uint16"),
    "pix": ("sbuf", [128, 1], "int32"),
    "cin": ("sbuf", [128, 2], "int32"),
    "cfl": ("sbuf", [128, 8], "float32"),
    "jj1": ("sbuf", [128, 256], "bfloat16"),
    "msk": ("sbuf", [128, 128], "float32"),
    "rpl": ("sbuf", [128, 128], "float32"),
    "iqq": ("sbuf", [128, TL], "float32"),
    "val": ("sbuf", [128, 256], "bfloat16"),
    "wgt": ("sbuf", [128, 8], "bfloat16"),
    "rr1": ("sbuf", [128, 128], "float32"),
    "lof": ("sbuf", [128, 128], "uint16"),
    "fof": ("sbuf", [128, TL], "uint16"),
    "px1": ("psum", [128, 512], "float32"),
    "pl1": ("psum", [128, 512], "float32"),
}
SEMAPHORES = ["ldx", "ldg", "gip", "gij", "gia", "gim", "giq", "vv", "pe", "p1", "q1", "q2", "q3", "hin", "sent", "st",
              "st2", "g1", "g2", "g3a", "g3b", "own", "y0", "y1"]


def _bits(m):
    return bin(m).count("1")


def _half(m):
    keep = _bits(m) // 2
    out = 0
    for b in range(16):
        if (m >> b) & 1 and keep > 0:
            out |= 1 << b
            keep -= 1
    return out


def _mask2(topo, src, dst, d):
    m = topo.mask(src, dst)
    return _half(m) if d % 2 == 1 else m & ~_half(m)


def _plan(T, topo):
    cores = list(T.cores)
    n = len(cores)
    plane0 = [r for r in range(n) if r == 0 or topo.same_plane(topo.chip(cores[0]), topo.chip(cores[r]))]
    plane1 = [r for r in range(n) if r not in plane0]
    grid = [[plane0[2 * R], plane1[2 * R], plane0[2 * R + 1], plane1[2 * R + 1]] for R in range(4)]
    plan = {}
    for R in range(4):
        for C in range(4):
            r = grid[R][C]
            c = cores[r]
            others = [grid[R][k] for k in range(4) if k != C]
            direct = [o for o in others if topo.may_write(c, cores[o])]
            relay = [o for o in others if o not in direct]
            helpers = []
            if relay:
                chip = topo.chip(c)
                cand = [h for h in range(128) if topo.chip(h) == chip and h != c
                        and all(topo.may_write(h, cores[o]) for o in relay)]
                cand.sort(key=lambda h: (topo.die(h) != topo.die(c), h))
                helpers = cand[:2]
            plan[r] = dict(R=R, C=C, direct=direct, relay=relay, helpers=helpers)
    return grid, plan


def _multi(T, topo, src_core, dst_ranks, ap, sem):
    cores = T.cores
    m = topo.mask(src_core, cores[dst_ranks[0]])
    ids = []
    for o in dst_ranks:
        m &= topo.mask(src_core, cores[o])
        rid, pid, _s = topo.addr(cores[o])
        ids.append(DstId(rid=rid, pnc=pid))
    return RemoteDMATransfer(dst_ids=ids, dma_engine_mask=m, remote_sem=sem, srcs=[ap],
                             dsts=[ap for _o in dst_ranks]), _bits(m)


def rank_program(g, core, T, topo):
    grid, plan = _plan(T, topo)
    cores = T.cores
    S = T.sem
    rank = T.rank_of(core)

    if rank is None:
        for r, pl in plan.items():
            for h, hc in enumerate(pl["helpers"]):
                if hc != core:
                    continue
                lo = topo.mask(cores[r], cores[pl["relay"][0]])
                inm = lo if h == 0 else topo.mask(cores[r], hc) & ~lo
                a = W * pl["C"] + (W // 2) * h
                tr, nb = _multi(T, topo, core, pl["relay"], T.win[:, a:a + W // 2], S.p1)
                g.wait_ge(S.hin, _bits(inm))
                g.remote_dma_fused([tr], local_sem=S.sent)
                g.wait_ge(S.sent, nb)
        return

    me = plan[rank]
    R, C = me["R"], me["C"]
    RL = (R + 1) % 4
    V = g.vector
    SC = g.scalar
    A = AluOpType
    nv = [0]

    def vop(inst, wait=True):
        inst.then_inc(S.vv, 1)
        nv[0] += 1
        if wait:
            V.wait_ge(S.vv, nv[0])
        return nv[0]

    own = T.win[:, W * C:W * C + W]
    g.sync.dma_start(own, T.x[:, :]).then_inc(S.ldx, 16)
    for grp in range(8):
        s = grid[R][grp >> 1]
        c0 = 32 * s + 16 * (grp & 1)
        q = g.scalar if grp % 2 == 0 else g.sync
        q.dma_start(T.gin[16 * grp:16 * grp + 16, :], T.goes[:, c0:c0 + 16]).then_inc(S.ldg, 16)

    g.iota(T.pix[:, 0:1], [[0, 1]], 0, 1).then_inc(S.gip, 1)
    g.iota(T.jj1[:, :], [[1, 256]], 1, 0, allow_small_or_imprecise_dtypes=True).then_inc(S.gij, 1)

    sent = 0
    g.wait_ge(S.ldx, 16)
    if me["relay"]:
        lo = topo.mask(core, cores[me["relay"][0]])
        trs = []
        for h, hc in enumerate(me["helpers"]):
            m = lo if h == 0 else topo.mask(core, hc) & ~lo
            rid, pid, _s = topo.addr(hc)
            a = W * C + (W // 2) * h
            trs.append(RemoteDMATransfer(dst_ids=[DstId(rid=rid, pnc=pid)], dma_engine_mask=m, remote_sem=S.hin,
                                         src=T.win[:, a:a + W // 2], dst=T.win[:, a:a + W // 2]))
            sent += _bits(m)
        g.remote_dma_fused(trs, local_sem=S.sent)
    tr, nb = _multi(T, topo, core, me["direct"], own, S.p1)
    g.remote_dma_fused([tr], local_sem=S.sent)
    sent += nb

    g.iota(T.msk[:, :], [[0, 16], [1, 8]], 0, 0, allow_small_or_imprecise_dtypes=True).then_inc(S.gia, 1)
    g.iota(T.rpl[:, :], [[0, 8], [1, 16]], 0, 0, allow_small_or_imprecise_dtypes=True).then_inc(S.gim, 1)
    g.iota(T.iqq[:, :], [[16, TL]], 0, 0, allow_small_or_imprecise_dtypes=True).then_inc(S.giq, 1)

    p1 = 0
    for k in range(4):
        o = grid[R][k]
        if o == rank:
            continue
        if rank in plan[o]["direct"]:
            p1 += _bits(topo.mask(cores[o], core))
        else:
            p1 += sum(_bits(topo.mask(hc, core)) for hc in plan[o]["helpers"])

    pg, pr, e0, e1, t0, s1 = (T.cfl[:, i:i + 1] for i in range(6))
    for Rp in range(4):
        a = W * grid[Rp][C]
        vop(V.memset(T.swn[:, a:a + W], 0.0), wait=False)
    V.wait_ge(S.gip, 1)
    vop(V.tensor_scalar(T.cin[:, 0:1], T.pix[:, 0:1], 4, None, A.arith_shift_right), wait=False)
    vop(V.tensor_scalar(T.cin[:, 1:2], T.pix[:, 0:1], 15, None, A.bitwise_and))
    vop(V.tensor_copy(pg, T.cin[:, 0:1]), wait=False)
    vop(V.tensor_copy(pr, T.cin[:, 1:2]))
    vop(V.tensor_scalar(e0, pr, 0.0, None, A.is_equal), wait=False)
    vop(V.tensor_scalar(e1, pr, 1.0, None, A.is_equal))
    V.wait_ge(S.gij, 1)
    vop(V.tensor_scalar(T.val[:, :], T.jj1[:, :], e0, e1, A.mult, A.add), wait=False)
    vop(V.tensor_scalar(t0, pg, 256.0, e1, A.mult, A.mult))
    vop(V.tensor_tensor(s1, t0, e0, A.add))
    vop(V.tensor_scalar(T.wgt[:, :], T.jj1[:, 0:8], 0.0, s1, A.mult, A.add), wait=False)
    V.wait_ge(S.ldg, 128)
    vop(V.tensor_copy(T.gof[:, :], T.gin[:, :]))
    n_sc = vop(V.tensor_copy(T.swn[:, 0:16 * W].indirect(T.gof[:, 0:16]), T.val[:, :]))
    V.wait_ge(S.gia, 1)
    vop(V.tensor_scalar(T.msk[:, :], T.msk[:, :], pg, None, A.is_equal), wait=False)
    V.wait_ge(S.gim, 1)
    vop(V.tensor_scalar(T.rpl[:, :], T.rpl[:, :], pr, None, A.is_equal), wait=False)
    V.wait_ge(S.giq, 1)
    vop(V.tensor_scalar(T.iqq[:, :], T.iqq[:, :], pr, float(MW * RL), A.add, A.add))

    g.tensor.wait_ge(S.vv, n_sc)
    for Rp in range(4):
        for u4 in range(4):
            u = 4 * Rp + u4
            a = W * grid[Rp][C] + 128 * u4
            g.tensor.matmul(T.px1[:, 8 * u:8 * u + 8], T.swn[:, a:a + 128], T.wgt[:, :], True, True).then_inc(S.pe, 1)
    V.wait_ge(S.pe, 16)
    n_r1 = vop(V.tensor_tensor(T.rr1[:, :], T.px1[:, 0:128], T.msk[:, :], A.mult))
    g.tensor.wait_ge(S.vv, n_r1)
    g.tensor.matmul(T.pl1[:, 0:128], T.rpl[:, :], T.rr1[:, :], True, True).then_inc(S.pe, 1)
    V.wait_ge(S.pe, 17)

    def tail(out, Rp):
        return V.tensor_scalar(out, T.pl1[:, TL * Rp:TL * Rp + TL], 0.5, float(MW * (R - (Rp + 1) % 4)),
                               A.is_gt, A.mult)

    vop(V.tensor_scalar(T.lof[:, :], T.pl1[:, 0:128], -1.0, 0.0, A.add, A.max), wait=False)
    vop(tail(T.snd[:, W:MW], (R + 1) % 4), wait=False)
    vop(tail(T.snd[:, MW + W:2 * MW], (R + 2) % 4), wait=False)
    a = MW * R + W
    vop(V.memset(T.cnd[:, MW * RL + W:MW * RL + MW], 0.0), wait=False)
    n_l = vop(tail(T.cnd[:, a:a + TL], R))
    vop(V.tensor_tensor(T.iqq[:, :], T.iqq[:, :], T.cnd[:, a:a + TL], A.add))

    H, HT = W // 2, TL // 2
    win = T.win[:, 0:4 * W]

    def sgather(out, window, off, sem):
        SC.activation(out, window.indirect(off), ActivationFunctionType.Copy, bias=-0.0, scale=1.0).then_inc(sem, 1)

    R1, R2, R3 = (R + 1) % 4, (R + 2) % 4, (R + 3) % 4
    V.wait_ge(S.ldx, 16)
    V.wait_ge(S.p1, p1)
    V.tensor_copy(T.snd[:, 0:W], win.indirect(T.lof[:, TL * R1:TL * R1 + TL])).then_inc(S.g1, 1)
    V.tensor_copy(T.snd[:, 2 * MW:2 * MW + H], win.indirect(T.lof[:, TL * R3:TL * R3 + HT])).then_inc(S.g3a, 1)
    SC.wait_ge(S.vv, n_l)
    SC.wait_ge(S.ldx, 16)
    SC.wait_ge(S.p1, p1)
    sgather(T.snd[:, MW:MW + W], win, T.lof[:, TL * R2:TL * R2 + TL], S.g2)
    sgather(T.snd[:, 2 * MW + H:2 * MW + W], win, T.lof[:, TL * R3 + HT:TL * R3 + TL], S.g3b)
    sgather(T.cnd[:, MW * R:MW * R + W], win, T.lof[:, TL * R:TL * R + TL], S.own)

    for rdy, Rp, a, b, w, d, q in ((S.g1, R1, 0, 0, MW, 1, S.q1), (S.g2, R2, MW, 0, MW, 2, S.q2),
                                   (S.g3a, R3, 2 * MW, 0, H, 3, S.q3), (S.g3b, R3, 2 * MW + H, H, H, 4, S.q3)):
        dst = cores[grid[Rp][C]]
        rid, pid, _s = topo.addr(dst)
        m = _mask2(topo, core, dst, d)
        g.wait_ge(rdy, 1)
        g.remote_dma(out_ap=T.cnd[:, MW * R + b:MW * R + b + w], in_ap=T.snd[:, a:a + w], remote_sem=q,
                     local_sem=S.sent, pid=pid, routing_id=rid, dma_engine_mask=m)
        sent += _bits(m)

    nq = {}
    for d in (1, 2):
        Rs = (R - d) % 4
        nq[d] = _bits(_mask2(topo, cores[grid[Rs][C]], core, d))
        V.wait_ge(S["q%d" % d], nq[d])
        a = MW * Rs + W
        vop(V.tensor_tensor(T.iqq[:, :], T.iqq[:, :], T.cnd[:, a:a + TL], A.add))
    n_f = vop(V.tensor_copy(T.fof[:, :], T.iqq[:, :]))
    nq[3] = _bits(_mask2(topo, cores[grid[RL][C]], core, 3)) + _bits(_mask2(topo, cores[grid[RL][C]], core, 4))
    cnd = T.cnd[:, 0:4 * MW]
    V.wait_ge(S.q3, nq[3])
    V.wait_ge(S.own, 1)
    V.tensor_copy(T.ysb[:, 0:H], cnd.indirect(T.fof[:, 0:HT])).then_inc(S.y0, 1)
    g.sync.wait_ge(S.y0, 1)
    g.sync.dma_start(T.y[:, 0:H], T.ysb[:, 0:H]).then_inc(S.st, 16)
    g.sync.wait_ge(S.st, 16)
    SC.wait_ge(S.vv, n_f)
    for d in (1, 2, 3):
        SC.wait_ge(S["q%d" % d], nq[d])
    SC.wait_ge(S.own, 1)
    sgather(T.ysb[:, H:W], cnd, T.fof[:, HT:TL], S.y1)
    SC.wait_ge(S.y1, 1)
    SC.dma_start(T.y[:, H:W], T.ysb[:, H:W]).then_inc(S.st2, 16)
    SC.wait_ge(S.st2, 16)
    g.wait_ge(S.sent, sent)
